import numpy as np, ml_dtypes
CORES = [17,81,89,18,82,90]
N = 6
W, KW, DIL = 512, 5, 1
H = (KW // 2) * DIL
def setup_inputs(rng):
    return {"x": rng.standard_normal((N, 128, W), dtype=np.float32).astype(ml_dtypes.bfloat16), "w": rng.standard_normal((N, 128, KW * 128), dtype=np.float32).astype(ml_dtypes.bfloat16)}
def setup_inputs_big(rng):
    d = setup_inputs(rng)
    for k in ("x", "w"): d[k] = (d[k].astype(np.float32) * 1024.0).astype(d[k].dtype)
    return d
def setup_inputs_small(rng):
    d = setup_inputs(rng)
    for k in ("x", "w"): d[k] = (d[k].astype(np.float32) * (1 / 1024.0)).astype(d[k].dtype)
    return d
def reference(x, w):
    X, W_ = x.astype(np.float64), w.astype(np.float64)
    g = np.concatenate(list(X), axis=1)
    p = np.concatenate([g[:, -H:], g, g[:, :H]], axis=1)
    y = np.zeros((N, 128, W))
    for r in range(N):
        for i in range(KW):
            y[r] += W_[r][:, 128 * i:128 * i + 128].T @ p[:, W * r + i * DIL:W * r + i * DIL + W]
    return {"y": y.astype(ml_dtypes.bfloat16 if x.dtype != np.float64 else np.float64)}

@@ -1,0 +1,158 @@
+from concourse.bass import DstId, RemoteDMATransfer
+
+P, WID, KW, H = 128, 512, 5, 2
+OFF = 2 * H
+BF = "bfloat16"
+SCRATCH = {
+    "xp": ("sbuf", [P, WID + 4 * H], BF),
+    "ws": ("sbuf", [P, KW * P], BF),
+    "yi": ("sbuf", [P, WID - 2 * H], BF),
+    "yl": ("sbuf", [P, H], BF),
+    "yr": ("sbuf", [P, H], BF),
+    "e4": ("dram", [P, 2 * H], BF),
+    "rb": ("dram", [P, 2 * H], BF),
+    "nl": ("dram", [P, 2 * H], BF),
+    "nr": ("dram", [P, 2 * H], BF),
+    "pi": ("psum", [P, 512], "float32"),
+    "pl": ("psum", [P, 512], "float32"),
+    "pr": ("psum", [P, 512], "float32"),
+}
+SEMAPHORES = ["edge", "ldx", "ldw", "sent", "relay", "nl", "nr", "hl", "hr",
+              "mi", "ml", "mr", "ci", "cl", "cr", "st"]
+
+
+def _flows(cores, topo):
+    n, out = len(cores), []
+    for r, c in enumerate(cores):
+        for side, d in (("r", cores[(r - 1) % n]), ("l", cores[(r + 1) % n])):
+            via = None
+            if not topo.may_write(c, d):
+                cand = [k for k in cores if k not in (c, d) and topo.chip(k) == topo.chip(c) and topo.may_write(k, d)]
+                cand.sort(key=lambda k: topo.die(k) != topo.die(c))
+                via = cand[0]
+            out.append((c, d, side, via))
+    return out
+
+
+def _pow2(n):
+    p = 1
+    while 2 * p <= n:
+        p *= 2
+    return p
+
+
+def _calls(flows, topo, c):
+    hops, direct = [], []
+    for s, d, side, via in flows:
+        if s == c and via is None:
+            direct.append((d, side))
+        elif s == c and via not in hops:
+            hops.append(via)
+    fwd = [(d, side) for s, d, side, via in flows if via == c]
+    own = [(d, "hop") for d in hops] + direct
+    common = -1
+    for d, _ in own + fwd:
+        common &= topo.mask(c, d)
+    bits = [b for b in range(common.bit_length()) if (common >> b) & 1]
+
+    def deal(items, each):
+        res = []
+        for i, (d, kind) in enumerate(items):
+            m = 0
+            for b in bits[i * each:(i + 1) * each]:
+                m |= 1 << b
+            res.append((d, kind, m, each))
+        return res
+    return (deal(own, _pow2(len(bits) // len(own)) if fwd else 1),
+            deal(fwd, _pow2(len(bits) // len(fwd))) if fwd else [])
+
+
+def rank_program(g, core, T, topo):
+    if T.rank_of(core) is None:
+        return
+    S = T.sem
+    flows = _flows(list(T.cores), topo)
+    own, fwd = _calls(flows, topo, core)
+    q = {"l": g.sync, "r": g.scalar}
+    land = {"l": T.xp[:, 0:2 * H], "r": T.xp[:, OFF + WID:OFF + WID + 2 * H]}
+    strip = {"l": T.nl, "r": T.nr}
+    s_strip, s_halo = {"l": S.nl, "r": S.nr}, {"l": S.hl, "r": S.hr}
+
+    come = {}
+    for s, d, side, via in flows:
+        if d == core:
+            calls = _calls(flows, topo, s if via is None else via)
+            lst = calls[0] if via is None else calls[1]
+            eng = [e for dd, kind, m, e in lst if dd == core and kind == side][0]
+            come[side] = (via is not None, eng, bool(calls[1]))
+    order = sorted(("l", "r"), key=lambda sd: (come[sd][0], come[sd][2]))
+    late = order[1]
+
+    g.sync.dma_start(T.e4[:, 0:H], T.x[:, 0:H]).then_inc(S.edge, 16)
+    g.scalar.dma_start(T.e4[:, H:2 * H], T.x[:, WID - H:WID]).then_inc(S.edge, 16)
+    g.sync.dma_start(T.xp[:, OFF:OFF + WID], T.x[:]).then_inc(S.ldx, 16)
+    g.scalar.dma_start(T.ws[:], T.w[:]).then_inc(S.ldw, 16)
+
+    def send(items, src, dst_of, sem_of):
+        tr = []
+        for d, kind, m, e in items:
+            rid, pid, _ = topo.addr(d)
+            tr.append(RemoteDMATransfer(dst_ids=[DstId(rid=rid, pnc=pid)], dma_engine_mask=m,
+                                        remote_sem=sem_of[kind], src=src, dst=dst_of[kind]))
+        g.remote_dma_fused(tr, local_sem=S.sent)
+        return sum(e for _, _, _, e in items)
+
+    g.wait_ge(S.edge, 32)
+    sent = send(own, T.e4[:], {"hop": T.rb[:], "l": T.nl[:], "r": T.nr[:]}, {"hop": S.relay, "l": S.nl, "r": S.nr})
+    if fwd:
+        srcs = sorted(set(s for s, d, side, via in flows if via == core))
+        assert len(srcs) == 1
+        hop = [e for d, kind, m, e in _calls(flows, topo, srcs[0])[0] if d == core and kind == "hop"][0]
+        g.wait_ge(S.relay, hop)
+        sent += send(fwd, T.rb[:], land, s_halo)
+
+    def tap(i):
+        return T.ws[:, P * i:P * i + P]
+
+    te = g.tensor
+    te.wait_ge(S.ldx, 16)
+    te.wait_ge(S.ldw, 16)
+    nin = WID - 2 * H
+    for i in range(KW):
+        mm = te.matmul(T.pi[:, 0:nin], tap(i), T.xp[:, OFF + i:OFF + i + nin], i == 0, i == KW - 1)
+    mm.then_inc(S.mi, 1)
+    base = {"l": OFF - H, "r": OFF + WID - 2 * H}
+    bank = {"l": T.pl, "r": T.pr}
+    alone = {"l": [2, 3, 4], "r": [2, 1, 0]}
+    halo = {"l": [0, 1], "r": [4, 3]}
+    s_mm = {"l": S.ml, "r": S.mr}
+    s_cp = {"l": S.cl, "r": S.cr}
+    for sd in order:
+        for n_, i in enumerate(alone[sd]):
+            te.matmul(bank[sd][:, 0:H], tap(i), T.xp[:, base[sd] + i:base[sd] + i + H], n_ == 0, False)
+    for sd in order:
+        te.wait_ge(s_halo[sd], come[sd][1] if come[sd][0] else 16)
+        for n_, i in enumerate(halo[sd]):
+            mm = te.matmul(bank[sd][:, 0:H], tap(i), T.xp[:, base[sd] + i:base[sd] + i + H], False, n_ == 1)
+        mm.then_inc(s_mm[sd], 1)
+
+    ve = g.vector
+    ybuf = {"l": T.yl, "r": T.yr}
+    ve.wait_ge(S.mi, 1)
+    ve.tensor_copy(T.yi[:], T.pi[:, 0:nin]).then_inc(S.ci, 1)
+    for sd in order:
+        ve.wait_ge(s_mm[sd], 1)
+        ve.tensor_copy(ybuf[sd][:], bank[sd][:, 0:H]).then_inc(s_cp[sd], 1)
+
+    q[late].wait_ge(S.ci, 1)
+    q[late].dma_start(T.y[:, H:WID - H], T.yi[:]).then_inc(S.st, 16)
+    ycol = {"l": T.y[:, 0:H], "r": T.y[:, WID - H:WID]}
+    for sd in order:
+        if not come[sd][0]:
+            q[sd].wait_ge(s_strip[sd], come[sd][1])
+            q[sd].dma_start(land[sd], strip[sd][:]).then_inc(s_halo[sd], 16)
+        q[sd].wait_ge(s_cp[sd], 1)
+        q[sd].dma_start(ycol[sd], ybuf[sd][:]).then_inc(S.st, 16)
+
+    g.wait_ge(S.sent, sent)
+    g.wait_ge(S.st, 48)

@@ -1,36 +1,40 @@
 from concourse.bass import DstId, RemoteDMATransfer
 
 P, WID, KW, H = 128, 512, 5, 2
-OFF = 2 * H
+BW = 64
+MID = WID // 2
+XS = MID + H
 BF = "bfloat16"
 SCRATCH = {
-    "xp": ("sbuf", [P, WID + 4 * H], BF),
+    "xp": ("sbuf", [P, WID + 2 * H], BF),
     "ws": ("sbuf", [P, KW * P], BF),
-    "yi": ("sbuf", [P, WID - 2 * H], BF),
-    "yl": ("sbuf", [P, H], BF),
-    "yr": ("sbuf", [P, H], BF),
-    "e4": ("dram", [P, 2 * H], BF),
-    "rb": ("dram", [P, 2 * H], BF),
-    "nl": ("dram", [P, 2 * H], BF),
-    "nr": ("dram", [P, 2 * H], BF),
-    "pi": ("psum", [P, 512], "float32"),
+    "y1": ("sbuf", [P, MID - BW], BF),
+    "y2": ("sbuf", [P, MID - BW], BF),
+    "yl": ("sbuf", [P, BW], BF),
+    "yr": ("sbuf", [P, BW], BF),
+    "el": ("dram", [P, H], BF),
+    "er": ("dram", [P, H], BF),
+    "rbl": ("dram", [P, H], BF),
+    "rbr": ("dram", [P, H], BF),
+    "p1": ("psum", [P, 512], "float32"),
+    "p2": ("psum", [P, 512], "float32"),
     "pl": ("psum", [P, 512], "float32"),
     "pr": ("psum", [P, 512], "float32"),
 }
-SEMAPHORES = ["edge", "ldx", "ldw", "sent", "relay", "nl", "nr", "hl", "hr",
-              "mi", "ml", "mr", "ci", "cl", "cr", "st"]
+SEMAPHORES = ["el", "er", "xa", "xb", "wa", "wb", "sent", "rl", "rr", "hl", "hr",
+              "m1", "m2", "ml", "mr", "c1", "c2", "cl", "cr", "st"]
 
 
 def _flows(cores, topo):
     n, out = len(cores), []
     for r, c in enumerate(cores):
-        for side, d in (("r", cores[(r - 1) % n]), ("l", cores[(r + 1) % n])):
+        for edge, side, d in (("l", "r", cores[(r - 1) % n]), ("r", "l", cores[(r + 1) % n])):
             via = None
             if not topo.may_write(c, d):
                 cand = [k for k in cores if k not in (c, d) and topo.chip(k) == topo.chip(c) and topo.may_write(k, d)]
                 cand.sort(key=lambda k: topo.die(k) != topo.die(c))
                 via = cand[0]
-            out.append((c, d, side, via))
+            out.append((c, d, edge, side, via))
     return out
 
 
@@ -41,30 +45,47 @@ def _pow2(n):
     return p
 
 
-def _calls(flows, topo, c):
-    hops, direct = [], []
-    for s, d, side, via in flows:
-        if s == c and via is None:
-            direct.append((d, side))
-        elif s == c and via not in hops:
-            hops.append(via)
-    fwd = [(d, side) for s, d, side, via in flows if via == c]
-    own = [(d, "hop") for d in hops] + direct
+def _links(topo, a, b):
+    ca, cb = topo.chip(a), topo.chip(b)
+    if ca == cb:
+        return 0
+    return 1 if topo.mates(ca, cb) or topo.same_plane(ca, cb) else 2
+
+
+def _sending(flows, topo, s):
+    return sorted([f for f in flows if f[0] == s],
+                  key=lambda f: (f[4] is None, -_links(topo, f[0] if f[4] is None else f[4], f[1])))
+
+
+def _plan(flows, topo, c):
+    mine = _sending(flows, topo, c)
+    thru = [f for f in flows if f[4] == c]
     common = -1
-    for d, _ in own + fwd:
-        common &= topo.mask(c, d)
+    for f in mine:
+        common &= topo.mask(c, f[1] if f[4] is None else f[4])
+    for f in thru:
+        common &= topo.mask(c, f[1])
     bits = [b for b in range(common.bit_length()) if (common >> b) & 1]
 
-    def deal(items, each):
-        res = []
-        for i, (d, kind) in enumerate(items):
-            m = 0
-            for b in bits[i * each:(i + 1) * each]:
-                m |= 1 << b
-            res.append((d, kind, m, each))
-        return res
-    return (deal(own, _pow2(len(bits) // len(own)) if fwd else 1),
-            deal(fwd, _pow2(len(bits) // len(fwd))) if fwd else [])
+    def msk(lo, k):
+        m = 0
+        for b in bits[lo:lo + k]:
+            m |= 1 << b
+        return m
+    own = []
+    full = _pow2(len(bits))
+    each = _pow2(len(bits) // len(mine))
+    for i, f in enumerate(mine):
+        if thru:
+            own.append((f[2], f[3], f[1], False, msk(i * each, each), each))
+        elif f[4] is not None:
+            own.append((f[2], f[3], f[4], True, msk(0, 1), 1))
+        else:
+            own.append((f[2], f[3], f[1], False, msk(0, full), full))
+    fwd = []
+    for f in sorted(thru, key=lambda f: _sending(flows, topo, f[0]).index(f)):
+        fwd.append((f[3], f[1], msk(0, full), full))
+    return own, fwd
 
 
 def rank_program(g, core, T, topo):
@@ -72,87 +93,118 @@ def rank_program(g, core, T, topo):
         return
     S = T.sem
     flows = _flows(list(T.cores), topo)
-    own, fwd = _calls(flows, topo, core)
+    own, fwd = _plan(flows, topo, core)
     q = {"l": g.sync, "r": g.scalar}
-    land = {"l": T.xp[:, 0:2 * H], "r": T.xp[:, OFF + WID:OFF + WID + 2 * H]}
-    strip = {"l": T.nl, "r": T.nr}
-    s_strip, s_halo = {"l": S.nl, "r": S.nr}, {"l": S.hl, "r": S.hr}
+    land = {"l": T.xp[:, 0:H], "r": T.xp[:, H + WID:H + WID + H]}
+    rbuf = {"l": T.rbl, "r": T.rbr}
+    ebuf, s_edge = {"l": T.el, "r": T.er}, {"l": S.el, "r": S.er}
+    ecol = {"l": (0, H), "r": (WID - H, WID)}
+    s_halo, s_hop = {"l": S.hl, "r": S.hr}, {"l": S.rl, "r": S.rr}
 
-    come = {}
-    for s, d, side, via in flows:
+    come, hop_eng = {}, {}
+    for s, d, edge, side, via in flows:
         if d == core:
-            calls = _calls(flows, topo, s if via is None else via)
-            lst = calls[0] if via is None else calls[1]
-            eng = [e for dd, kind, m, e in lst if dd == core and kind == side][0]
-            come[side] = (via is not None, eng, bool(calls[1]))
-    order = sorted(("l", "r"), key=lambda sd: (come[sd][0], come[sd][2]))
-    late = order[1]
+            if via is None:
+                come[side] = ([o[5] for o in _plan(flows, topo, s)[0] if o[0] == edge][0], (0, 0))
+            else:
+                f = _plan(flows, topo, via)[1]
+                i = [n_ for n_, it in enumerate(f) if it[0] == side and it[1] == core][0]
+                come[side] = (f[i][3], (1, i))
+        if via == core:
+            hop_eng[side] = [o[5] for o in _plan(flows, topo, s)[0] if o[0] == edge][0]
+    order = sorted(("l", "r"), key=lambda sd: come[sd][1])
 
-    g.sync.dma_start(T.e4[:, 0:H], T.x[:, 0:H]).then_inc(S.edge, 16)
-    g.scalar.dma_start(T.e4[:, H:2 * H], T.x[:, WID - H:WID]).then_inc(S.edge, 16)
-    g.sync.dma_start(T.xp[:, OFF:OFF + WID], T.x[:]).then_inc(S.ldx, 16)
-    g.scalar.dma_start(T.ws[:], T.w[:]).then_inc(S.ldw, 16)
+    hp_ = P // 2
+    if fwd:
+        got = 16
+        for edge in ("l", "r"):
+            a, b = ecol[edge]
+            q[edge].dma_start(ebuf[edge][:], T.x[:, a:b]).then_inc(s_edge[edge], 16)
+    else:
+        got = 32
+        for edge in [o[0] for o in own]:
+            a, b = ecol[edge]
+            g.sync.dma_start(ebuf[edge][0:hp_, :], T.x[0:hp_, a:b]).then_inc(s_edge[edge], 16)
+            g.scalar.dma_start(ebuf[edge][hp_:P, :], T.x[hp_:P, a:b]).then_inc(s_edge[edge], 16)
+    g.sync.dma_start(T.xp[:, H:H + XS], T.x[:, 0:XS]).then_inc(S.xa, 16)
+    g.scalar.dma_start(T.ws[:, 2 * P:KW * P], T.w[:, 2 * P:KW * P]).then_inc(S.wa, 16)
+    g.sync.dma_start(T.xp[:, H + XS:H + WID], T.x[:, XS:WID]).then_inc(S.xb, 16)
+    g.scalar.dma_start(T.ws[:, 0:2 * P], T.w[:, 0:2 * P]).then_inc(S.wb, 16)
 
-    def send(items, src, dst_of, sem_of):
+    def send(items):
         tr = []
-        for d, kind, m, e in items:
+        for d, src, dst, sem, m, e in items:
             rid, pid, _ = topo.addr(d)
             tr.append(RemoteDMATransfer(dst_ids=[DstId(rid=rid, pnc=pid)], dma_engine_mask=m,
-                                        remote_sem=sem_of[kind], src=src, dst=dst_of[kind]))
+                                        remote_sem=sem, src=src, dst=dst))
         g.remote_dma_fused(tr, local_sem=S.sent)
-        return sum(e for _, _, _, e in items)
+        return sum(it[5] for it in items)
 
-    g.wait_ge(S.edge, 32)
-    sent = send(own, T.e4[:], {"hop": T.rb[:], "l": T.nl[:], "r": T.nr[:]}, {"hop": S.relay, "l": S.nl, "r": S.nr})
+    def item(o):
+        edge, side, t, hop, m, e = o
+        return (t, ebuf[edge][:], rbuf[side][:] if hop else land[side], (s_hop if hop else s_halo)[side], m, e)
+
+    sent = 0
     if fwd:
-        srcs = sorted(set(s for s, d, side, via in flows if via == core))
-        assert len(srcs) == 1
-        hop = [e for d, kind, m, e in _calls(flows, topo, srcs[0])[0] if d == core and kind == "hop"][0]
-        g.wait_ge(S.relay, hop)
-        sent += send(fwd, T.rb[:], land, s_halo)
-
-    def tap(i):
-        return T.ws[:, P * i:P * i + P]
+        for o in own:
+            g.wait_ge(s_edge[o[0]], got)
+        sent += send([item(o) for o in own])
+        for side, d, m, e in fwd:
+            g.wait_ge(s_hop[side], hop_eng[side])
+            sent += send([(d, rbuf[side][:], land[side], s_halo[side], m, e)])
+    else:
+        for o in own:
+            g.wait_ge(s_edge[o[0]], got)
+            sent += send([item(o)])
 
     te = g.tensor
-    te.wait_ge(S.ldx, 16)
-    te.wait_ge(S.ldw, 16)
-    nin = WID - 2 * H
-    for i in range(KW):
-        mm = te.matmul(T.pi[:, 0:nin], tap(i), T.xp[:, OFF + i:OFF + i + nin], i == 0, i == KW - 1)
-    mm.then_inc(S.mi, 1)
-    base = {"l": OFF - H, "r": OFF + WID - 2 * H}
+
+    def mm(bank, c0, c1, i, start, stop):
+        return te.matmul(bank[:, 0:c1 - c0], T.ws[:, P * i:P * i + P], T.xp[:, c0 + i:c1 + i], start, stop)
+
+    te.wait_ge(S.xa, 16)
+    te.wait_ge(S.wa, 16)
+    for i in (2, 3, 4):
+        mm(T.p1, BW, MID, i, i == 2, False)
+    for i in (2, 3, 4):
+        mm(T.pl, 0, BW, i, i == 2, False)
+    te.wait_ge(S.xb, 16)
+    for i in (2, 3, 4):
+        mm(T.p2, MID, WID - BW, i, i == 2, False)
+    mm(T.pr, WID - BW, WID, 2, True, False)
+    te.wait_ge(S.wb, 16)
+    mm(T.p1, BW, MID, 0, False, False)
+    mm(T.p1, BW, MID, 1, False, True).then_inc(S.m1, 1)
+    mm(T.p2, MID, WID - BW, 0, False, False)
+    mm(T.p2, MID, WID - BW, 1, False, True).then_inc(S.m2, 1)
+    mm(T.pr, WID - BW, WID, 0, False, False)
+    mm(T.pr, WID - BW, WID, 1, False, False)
     bank = {"l": T.pl, "r": T.pr}
-    alone = {"l": [2, 3, 4], "r": [2, 1, 0]}
-    halo = {"l": [0, 1], "r": [4, 3]}
-    s_mm = {"l": S.ml, "r": S.mr}
-    s_cp = {"l": S.cl, "r": S.cr}
+    span = {"l": (0, BW), "r": (WID - BW, WID)}
+    halo = {"l": (0, 1), "r": (3, 4)}
+    s_mm, s_cp = {"l": S.ml, "r": S.mr}, {"l": S.cl, "r": S.cr}
     for sd in order:
-        for n_, i in enumerate(alone[sd]):
-            te.matmul(bank[sd][:, 0:H], tap(i), T.xp[:, base[sd] + i:base[sd] + i + H], n_ == 0, False)
-    for sd in order:
-        te.wait_ge(s_halo[sd], come[sd][1] if come[sd][0] else 16)
-        for n_, i in enumerate(halo[sd]):
-            mm = te.matmul(bank[sd][:, 0:H], tap(i), T.xp[:, base[sd] + i:base[sd] + i + H], False, n_ == 1)
-        mm.then_inc(s_mm[sd], 1)
+        te.wait_ge(s_halo[sd], come[sd][0])
+        mm(bank[sd], span[sd][0], span[sd][1], halo[sd][0], False, False)
+        mm(bank[sd], span[sd][0], span[sd][1], halo[sd][1], False, True).then_inc(s_mm[sd], 1)
 
     ve = g.vector
     ybuf = {"l": T.yl, "r": T.yr}
-    ve.wait_ge(S.mi, 1)
-    ve.tensor_copy(T.yi[:], T.pi[:, 0:nin]).then_inc(S.ci, 1)
+    ve.wait_ge(S.m1, 1)
+    ve.tensor_copy(T.y1[:], T.p1[:, 0:MID - BW]).then_inc(S.c1, 1)
+    ve.wait_ge(S.m2, 1)
+    ve.tensor_copy(T.y2[:], T.p2[:, 0:MID - BW]).then_inc(S.c2, 1)
     for sd in order:
         ve.wait_ge(s_mm[sd], 1)
-        ve.tensor_copy(ybuf[sd][:], bank[sd][:, 0:H]).then_inc(s_cp[sd], 1)
+        ve.tensor_copy(ybuf[sd][:], bank[sd][:, 0:BW]).then_inc(s_cp[sd], 1)
 
-    q[late].wait_ge(S.ci, 1)
-    q[late].dma_start(T.y[:, H:WID - H], T.yi[:]).then_inc(S.st, 16)
-    ycol = {"l": T.y[:, 0:H], "r": T.y[:, WID - H:WID]}
+    q[order[0]].wait_ge(S.c1, 1)
+    q[order[0]].dma_start(T.y[:, BW:MID], T.y1[:]).then_inc(S.st, 16)
+    q[order[1]].wait_ge(S.c2, 1)
+    q[order[1]].dma_start(T.y[:, MID:WID - BW], T.y2[:]).then_inc(S.st, 16)
     for sd in order:
-        if not come[sd][0]:
-            q[sd].wait_ge(s_strip[sd], come[sd][1])
-            q[sd].dma_start(land[sd], strip[sd][:]).then_inc(s_halo[sd], 16)
         q[sd].wait_ge(s_cp[sd], 1)
-        q[sd].dma_start(ycol[sd], ybuf[sd][:]).then_inc(S.st, 16)
+        q[sd].dma_start(T.y[:, span[sd][0]:span[sd][1]], ybuf[sd][:]).then_inc(S.st, 16)
 
     g.wait_ge(S.sent, sent)
-    g.wait_ge(S.st, 48)
+    g.wait_ge(S.st, 64)

from concourse.bass import DstId, RemoteDMATransfer

P, WID, KW, H = 128, 512, 5, 2
BW = 64
MID = WID // 2
XS = MID + H
BF = "bfloat16"
SCRATCH = {
    "xp": ("sbuf", [P, WID + 2 * H], BF),
    "ws": ("sbuf", [P, KW * P], BF),
    "y1": ("sbuf", [P, MID - BW], BF),
    "y2": ("sbuf", [P, MID - BW], BF),
    "yl": ("sbuf", [P, BW], BF),
    "yr": ("sbuf", [P, BW], BF),
    "el": ("dram", [P, H], BF),
    "er": ("dram", [P, H], BF),
    "rbl": ("dram", [P, H], BF),
    "rbr": ("dram", [P, H], BF),
    "p1": ("psum", [P, 512], "float32"),
    "p2": ("psum", [P, 512], "float32"),
    "pl": ("psum", [P, 512], "float32"),
    "pr": ("psum", [P, 512], "float32"),
}
SEMAPHORES = ["el", "er", "xa", "xb", "wa", "wb", "sent", "rl", "rr", "hl", "hr",
              "m1", "m2", "ml", "mr", "c1", "c2", "cl", "cr", "st"]


def _flows(cores, topo):
    n, out = len(cores), []
    for r, c in enumerate(cores):
        for edge, side, d in (("l", "r", cores[(r - 1) % n]), ("r", "l", cores[(r + 1) % n])):
            via = None
            if not topo.may_write(c, d):
                cand = [k for k in cores if k not in (c, d) and topo.chip(k) == topo.chip(c) and topo.may_write(k, d)]
                cand.sort(key=lambda k: topo.die(k) != topo.die(c))
                via = cand[0]
            out.append((c, d, edge, side, via))
    return out


def _pow2(n):
    p = 1
    while 2 * p <= n:
        p *= 2
    return p


def _links(topo, a, b):
    ca, cb = topo.chip(a), topo.chip(b)
    if ca == cb:
        return 0
    return 1 if topo.mates(ca, cb) or topo.same_plane(ca, cb) else 2


def _sending(flows, topo, s):
    return sorted([f for f in flows if f[0] == s],
                  key=lambda f: (f[4] is None, -_links(topo, f[0] if f[4] is None else f[4], f[1])))


def _plan(flows, topo, c):
    mine = _sending(flows, topo, c)
    thru = [f for f in flows if f[4] == c]
    common = -1
    for f in mine:
        common &= topo.mask(c, f[1] if f[4] is None else f[4])
    for f in thru:
        common &= topo.mask(c, f[1])
    bits = [b for b in range(common.bit_length()) if (common >> b) & 1]

    def msk(lo, k):
        m = 0
        for b in bits[lo:lo + k]:
            m |= 1 << b
        return m
    own = []
    full = _pow2(len(bits))
    each = _pow2(len(bits) // len(mine))
    for i, f in enumerate(mine):
        if thru:
            own.append((f[2], f[3], f[1], False, msk(i * each, each), each))
        elif f[4] is not None:
            own.append((f[2], f[3], f[4], True, msk(0, 1), 1))
        else:
            own.append((f[2], f[3], f[1], False, msk(0, full), full))
    fwd = []
    for f in sorted(thru, key=lambda f: _sending(flows, topo, f[0]).index(f)):
        fwd.append((f[3], f[1], msk(0, full), full))
    return own, fwd


def rank_program(g, core, T, topo):
    if T.rank_of(core) is None:
        return
    S = T.sem
    flows = _flows(list(T.cores), topo)
    own, fwd = _plan(flows, topo, core)
    q = {"l": g.sync, "r": g.scalar}
    land = {"l": T.xp[:, 0:H], "r": T.xp[:, H + WID:H + WID + H]}
    rbuf = {"l": T.rbl, "r": T.rbr}
    ebuf, s_edge = {"l": T.el, "r": T.er}, {"l": S.el, "r": S.er}
    ecol = {"l": (0, H), "r": (WID - H, WID)}
    s_halo, s_hop = {"l": S.hl, "r": S.hr}, {"l": S.rl, "r": S.rr}

    come, hop_eng = {}, {}
    for s, d, edge, side, via in flows:
        if d == core:
            if via is None:
                come[side] = ([o[5] for o in _plan(flows, topo, s)[0] if o[0] == edge][0], (0, 0))
            else:
                f = _plan(flows, topo, via)[1]
                i = [n_ for n_, it in enumerate(f) if it[0] == side and it[1] == core][0]
                come[side] = (f[i][3], (1, i))
        if via == core:
            hop_eng[side] = [o[5] for o in _plan(flows, topo, s)[0] if o[0] == edge][0]
    order = sorted(("l", "r"), key=lambda sd: come[sd][1])

    hp_ = P // 2
    if fwd:
        got = 16
        for edge in ("l", "r"):
            a, b = ecol[edge]
            q[edge].dma_start(ebuf[edge][:], T.x[:, a:b]).then_inc(s_edge[edge], 16)
    else:
        got = 32
        for edge in [o[0] for o in own]:
            a, b = ecol[edge]
            g.sync.dma_start(ebuf[edge][0:hp_, :], T.x[0:hp_, a:b]).then_inc(s_edge[edge], 16)
            g.scalar.dma_start(ebuf[edge][hp_:P, :], T.x[hp_:P, a:b]).then_inc(s_edge[edge], 16)
    g.sync.dma_start(T.xp[:, H:H + XS], T.x[:, 0:XS]).then_inc(S.xa, 16)
    g.scalar.dma_start(T.ws[:, 2 * P:KW * P], T.w[:, 2 * P:KW * P]).then_inc(S.wa, 16)
    g.sync.dma_start(T.xp[:, H + XS:H + WID], T.x[:, XS:WID]).then_inc(S.xb, 16)
    g.scalar.dma_start(T.ws[:, 0:2 * P], T.w[:, 0:2 * P]).then_inc(S.wb, 16)

    def send(items):
        tr = []
        for d, src, dst, sem, m, e in items:
            rid, pid, _ = topo.addr(d)
            tr.append(RemoteDMATransfer(dst_ids=[DstId(rid=rid, pnc=pid)], dma_engine_mask=m,
                                        remote_sem=sem, src=src, dst=dst))
        g.remote_dma_fused(tr, local_sem=S.sent)
        return sum(it[5] for it in items)

    def item(o):
        edge, side, t, hop, m, e = o
        return (t, ebuf[edge][:], rbuf[side][:] if hop else land[side], (s_hop if hop else s_halo)[side], m, e)

    sent = 0
    if fwd:
        for o in own:
            g.wait_ge(s_edge[o[0]], got)
        sent += send([item(o) for o in own])
        for side, d, m, e in fwd:
            g.wait_ge(s_hop[side], hop_eng[side])
            sent += send([(d, rbuf[side][:], land[side], s_halo[side], m, e)])
    else:
        for o in own:
            g.wait_ge(s_edge[o[0]], got)
            sent += send([item(o)])

    te = g.tensor

    def mm(bank, c0, c1, i, start, stop):
        return te.matmul(bank[:, 0:c1 - c0], T.ws[:, P * i:P * i + P], T.xp[:, c0 + i:c1 + i], start, stop)

    te.wait_ge(S.xa, 16)
    te.wait_ge(S.wa, 16)
    for i in (2, 3, 4):
        mm(T.p1, BW, MID, i, i == 2, False)
    for i in (2, 3, 4):
        mm(T.pl, 0, BW, i, i == 2, False)
    te.wait_ge(S.xb, 16)
    for i in (2, 3, 4):
        mm(T.p2, MID, WID - BW, i, i == 2, False)
    mm(T.pr, WID - BW, WID, 2, True, False)
    te.wait_ge(S.wb, 16)
    mm(T.p1, BW, MID, 0, False, False)
    mm(T.p1, BW, MID, 1, False, True).then_inc(S.m1, 1)
    mm(T.p2, MID, WID - BW, 0, False, False)
    mm(T.p2, MID, WID - BW, 1, False, True).then_inc(S.m2, 1)
    mm(T.pr, WID - BW, WID, 0, False, False)
    mm(T.pr, WID - BW, WID, 1, False, False)
    bank = {"l": T.pl, "r": T.pr}
    span = {"l": (0, BW), "r": (WID - BW, WID)}
    halo = {"l": (0, 1), "r": (3, 4)}
    s_mm, s_cp = {"l": S.ml, "r": S.mr}, {"l": S.cl, "r": S.cr}
    for sd in order:
        te.wait_ge(s_halo[sd], come[sd][0])
        mm(bank[sd], span[sd][0], span[sd][1], halo[sd][0], False, False)
        mm(bank[sd], span[sd][0], span[sd][1], halo[sd][1], False, True).then_inc(s_mm[sd], 1)

    ve = g.vector
    ybuf = {"l": T.yl, "r": T.yr}
    ve.wait_ge(S.m1, 1)
    ve.tensor_copy(T.y1[:], T.p1[:, 0:MID - BW]).then_inc(S.c1, 1)
    ve.wait_ge(S.m2, 1)
    ve.tensor_copy(T.y2[:], T.p2[:, 0:MID - BW]).then_inc(S.c2, 1)
    for sd in order:
        ve.wait_ge(s_mm[sd], 1)
        ve.tensor_copy(ybuf[sd][:], bank[sd][:, 0:BW]).then_inc(s_cp[sd], 1)

    q[order[0]].wait_ge(S.c1, 1)
    q[order[0]].dma_start(T.y[:, BW:MID], T.y1[:]).then_inc(S.st, 16)
    q[order[1]].wait_ge(S.c2, 1)
    q[order[1]].dma_start(T.y[:, MID:WID - BW], T.y2[:]).then_inc(S.st, 16)
    for sd in order:
        q[sd].wait_ge(s_cp[sd], 1)
        q[sd].dma_start(T.y[:, span[sd][0]:span[sd][1]], ybuf[sd][:]).then_inc(S.st, 16)

    g.wait_ge(S.sent, sent)
    g.wait_ge(S.st, 64)
